import numpy as np, ml_dtypes
CORES = [4,12,20,28,44,60,76,84,92,108,116,124]
N = 12
F = 32
def setup_inputs(rng):
    return {"a": rng.standard_normal((N, 128, 128), dtype=np.float32).astype(ml_dtypes.bfloat16), "b": rng.standard_normal((N, 128, F), dtype=np.float32).astype(ml_dtypes.bfloat16)}
def setup_inputs_big(rng):
    d = setup_inputs(rng)
    for k in ("a", "b"): d[k] = (d[k].astype(np.float32) * 1024.0).astype(d[k].dtype)
    return d
def setup_inputs_small(rng):
    d = setup_inputs(rng)
    for k in ("a", "b"): d[k] = (d[k].astype(np.float32) * (1 / 1024.0)).astype(d[k].dtype)
    return d
def setup_inputs_apart(rng):
    d = setup_inputs(rng)
    f = (10.0 ** rng.permutation(np.linspace(-1.5, 1.5, N))).astype(np.float32).reshape(N, 1, 1)
    for k in ("a", "b"): d[k] = (d[k].astype(np.float32) * f).astype(d[k].dtype)
    return d
def reference(a, b):
    s = (a.astype(np.float64).sum(axis=0).T @ b.astype(np.float64).sum(axis=0)).astype(ml_dtypes.bfloat16 if a.dtype != np.float64 else np.float64)
    return {"y": np.broadcast_to(s, (N,) + s.shape)}

@@ -1,0 +1,150 @@
+from concourse.bass import DstId, RemoteDMATransfer
+
+KDIM, MDIM, FDIM = 128, 128, 32
+W = 32
+PA = KDIM * MDIM // (128 * W)
+PB = KDIM * FDIM // (128 * W)
+P = PA + PB
+RPP = 2
+Q = KDIM // RPP
+HUB_TRANSFERS = 4
+HUB_ENGINES = 1
+MAXSRC = 8
+
+SCRATCH = {
+    "stage": ("dram", [P, 128, W], "bfloat16"),
+    "hin": ("dram", [MAXSRC, 128, W], "bfloat16"),
+    "land": ("dram", [2 * P, 128, W], "bfloat16"),
+    "sa": ("sbuf", [128, 2 * RPP * MDIM], "bfloat16"),
+    "sb": ("sbuf", [128, 2 * RPP * FDIM], "bfloat16"),
+    "ys": ("sbuf", [128, FDIM], "bfloat16"),
+    "ps": ("psum", [128, FDIM], "float32"),
+}
+SEMAPHORES = ["ld", "sent", "got", "arr0", "arr1", "in0", "in1", "mm", "cp", "st"]
+
+
+def _bits(mask):
+    return [e for e in range(mask.bit_length()) if (mask >> e) & 1]
+
+
+def _spread(es):
+    return es[0::2] + es[1::2]
+
+
+def _dst(topo, c):
+    rid, pid, _ = topo.addr(c)
+    return DstId(rid=rid, pnc=pid)
+
+
+def _plan(T, topo):
+    ranks = list(T.cores)
+    classes = []
+    for r in ranks:
+        for cl in classes:
+            if topo.may_write(cl[0], r) and topo.may_write(r, cl[0]):
+                cl.append(r)
+                break
+        else:
+            classes.append([r])
+
+    def pair(ch):
+        for o in range(topo.CHIPS):
+            if topo.mates(ch, o):
+                return min(ch, o)
+        return ch
+
+    slots, dies, hubs = [], {}, []
+    for cl in classes:
+        cand = [c for c in range(topo.CHIPS * topo.CORES_PER_CHIP)
+                if c not in ranks
+                and all(topo.may_write(s, c) for s in cl)
+                and all(topo.may_write(c, d) for d in ranks)]
+        row, chips = [], []
+        for _t in range(P):
+            best = min((c for c in cand if c not in row),
+                       key=lambda c: ((pair(topo.chip(c)), topo.die(c)) in slots,
+                                      topo.chip(c) in chips,
+                                      sum(1 for u in slots if u[0] == pair(topo.chip(c))),
+                                      dies.get(topo.die(c), 0), c))
+            row.append(best)
+            chips.append(topo.chip(best))
+            slots.append((pair(topo.chip(best)), topo.die(best)))
+            dies[topo.die(best)] = dies.get(topo.die(best), 0) + 1
+        hubs.append(row)
+    return ranks, classes, hubs
+
+
+def _hub(g, core, T, topo, ranks, cl, x, t):
+    allowed = topo.mask(core, ranks[0])
+    for d in ranks:
+        allowed &= topo.mask(core, d)
+    es = _spread(_bits(allowed))
+    g.wait_ge(T.sem.got, len(cl))
+    trs = []
+    for i in range(HUB_TRANSFERS):
+        grp = ranks[i::HUB_TRANSFERS]
+        m = 0
+        for e in es[i * HUB_ENGINES:(i + 1) * HUB_ENGINES]:
+            m |= 1 << e
+        trs.append(RemoteDMATransfer(
+            dst_ids=[_dst(topo, d) for d in grp], dma_engine_mask=m, remote_sem=T.sem["arr%d" % x],
+            srcs=[T.hin[i2] for i2 in range(len(cl))], dsts=[T.land[x * P + t] for _d in grp], alu_op=1))
+    g.remote_dma_fused(trs, local_sem=T.sem.sent)
+    g.wait_ge(T.sem.sent, HUB_TRANSFERS * HUB_ENGINES)
+
+
+def _rank(g, core, T, topo, classes, hubs):
+    x = [i for i, cl in enumerate(classes) if core in cl][0]
+    me = classes[x].index(core)
+    queues = [g.sync, g.scalar]
+
+    g.sync.dma_start(T.stage[0:PA], T.a[:, :]).then_inc(T.sem.ld, 16)
+    g.scalar.dma_start(T.stage[PA:P], T.b[:, :]).then_inc(T.sem.ld, 16)
+
+    g.wait_ge(T.sem.ld, 32)
+    allowed = topo.mask(core, hubs[x][0])
+    for h in hubs[x]:
+        allowed &= topo.mask(core, h)
+    es = _spread(_bits(allowed))
+    g.remote_dma_fused(
+        [RemoteDMATransfer(dst_ids=[_dst(topo, h)], dma_engine_mask=1 << es[t], remote_sem=T.sem.got,
+                           src=T.stage[t], dst=T.hin[me])
+         for t, h in enumerate(hubs[x])],
+        local_sem=T.sem.sent)
+
+    wa, wb = RPP * MDIM, RPP * FDIM
+    for c, q in enumerate(queues):
+        q.wait_ge(T.sem["arr%d" % c], P * HUB_ENGINES)
+        q.dma_start(T.sa[0:Q, c * wa:(c + 1) * wa], T.land[c * P:c * P + PA]).then_inc(T.sem["in%d" % c], 16)
+        q.dma_start(T.sb[0:Q, c * wb:(c + 1) * wb], T.land[c * P + PA:(c + 1) * P]).then_inc(T.sem["in%d" % c], 16)
+
+    terms = [(0, 0), (0, 1), (1, 0), (1, 1)]
+    g.tensor.wait_ge(T.sem.in0, 32)
+    n, last = 0, len(terms) * RPP
+    for (ca, cb) in terms:
+        if (ca, cb) == (0, 1):
+            g.tensor.wait_ge(T.sem.in1, 32)
+        for s in range(RPP):
+            n += 1
+            mm = g.tensor.matmul(T.ps[:, :],
+                                 T.sa[0:Q, ca * wa + s * MDIM:ca * wa + (s + 1) * MDIM],
+                                 T.sb[0:Q, cb * wb + s * FDIM:cb * wb + (s + 1) * FDIM],
+                                 n == 1, n == last)
+    mm.then_inc(T.sem.mm, 1)
+
+    g.vector.wait_ge(T.sem.mm, 1)
+    g.vector.tensor_copy(T.ys[:, :], T.ps[:, :]).then_inc(T.sem.cp, 1)
+    g.sync.wait_ge(T.sem.cp, 1)
+    g.sync.dma_start(T.y[:, :], T.ys[:, :]).then_inc(T.sem.st, 16)
+    g.sync.wait_ge(T.sem.st, 16)
+    g.wait_ge(T.sem.sent, P)
+
+
+def rank_program(g, core, T, topo):
+    ranks, classes, hubs = _plan(T, topo)
+    if T.rank_of(core) is not None:
+        _rank(g, core, T, topo, classes, hubs)
+        return
+    for x, row in enumerate(hubs):
+        if core in row:
+            _hub(g, core, T, topo, ranks, classes[x], x, row.index(core))

@@ -1,7 +1,7 @@
 from concourse.bass import DstId, RemoteDMATransfer
 
 KDIM, MDIM, FDIM = 128, 128, 32
-W = 32
+W = 16
 PA = KDIM * MDIM // (128 * W)
 PB = KDIM * FDIM // (128 * W)
 P = PA + PB
@@ -9,6 +9,7 @@ RPP = 2
 Q = KDIM // RPP
 HUB_TRANSFERS = 4
 HUB_ENGINES = 1
+RANK_TRANSFERS = 5
 MAXSRC = 8
 
 SCRATCH = {
@@ -62,8 +63,8 @@ def _plan(T, topo):
         row, chips = [], []
         for _t in range(P):
             best = min((c for c in cand if c not in row),
-                       key=lambda c: ((pair(topo.chip(c)), topo.die(c)) in slots,
-                                      topo.chip(c) in chips,
+                       key=lambda c: (slots.count((pair(topo.chip(c)), topo.die(c))),
+                                      chips.count(topo.chip(c)),
                                       sum(1 for u in slots if u[0] == pair(topo.chip(c))),
                                       dies.get(topo.die(c), 0), c))
             row.append(best)
@@ -106,11 +107,12 @@ def _rank(g, core, T, topo, classes, hubs):
     for h in hubs[x]:
         allowed &= topo.mask(core, h)
     es = _spread(_bits(allowed))
-    g.remote_dma_fused(
-        [RemoteDMATransfer(dst_ids=[_dst(topo, h)], dma_engine_mask=1 << es[t], remote_sem=T.sem.got,
-                           src=T.stage[t], dst=T.hin[me])
-         for t, h in enumerate(hubs[x])],
-        local_sem=T.sem.sent)
+    for t0 in range(0, P, RANK_TRANSFERS):
+        g.remote_dma_fused(
+            [RemoteDMATransfer(dst_ids=[_dst(topo, hubs[x][t])], dma_engine_mask=1 << es[t - t0],
+                               remote_sem=T.sem.got, src=T.stage[t], dst=T.hin[me])
+             for t in range(t0, min(P, t0 + RANK_TRANSFERS))],
+            local_sem=T.sem.sent)
 
     wa, wb = RPP * MDIM, RPP * FDIM
     for c, q in enumerate(queues):

@@ -1,7 +1,7 @@
 from concourse.bass import DstId, RemoteDMATransfer
 
 KDIM, MDIM, FDIM = 128, 128, 32
-W = 16
+W = 8
 PA = KDIM * MDIM // (128 * W)
 PB = KDIM * FDIM // (128 * W)
 P = PA + PB

@@ -1,4 +1,5 @@
 from concourse.bass import DstId, RemoteDMATransfer
+from concourse.mybir import AluOpType
 
 KDIM, MDIM, FDIM = 128, 128, 32
 W = 8
@@ -8,8 +9,6 @@ P = PA + PB
 RPP = 2
 Q = KDIM // RPP
 HUB_TRANSFERS = 4
-HUB_ENGINES = 1
-RANK_TRANSFERS = 5
 MAXSRC = 8
 
 SCRATCH = {
@@ -18,10 +17,12 @@ SCRATCH = {
     "land": ("dram", [2 * P, 128, W], "bfloat16"),
     "sa": ("sbuf", [128, 2 * RPP * MDIM], "bfloat16"),
     "sb": ("sbuf", [128, 2 * RPP * FDIM], "bfloat16"),
+    "sbs": ("sbuf", [128, RPP * FDIM], "bfloat16"),
     "ys": ("sbuf", [128, FDIM], "bfloat16"),
     "ps": ("psum", [128, FDIM], "float32"),
 }
-SEMAPHORES = ["ld", "sent", "got", "arr0", "arr1", "in0", "in1", "mm", "cp", "st"]
+SEMAPHORES = ["lda", "ldb", "sent", "got", "arra0", "arra1", "arrb0", "arrb1",
+              "ina0", "ina1", "inb0", "inb1", "bs", "mm", "cp", "st"]
 
 
 def _bits(mask):
@@ -35,6 +36,13 @@ def _spread(es):
 def _dst(topo, c):
     rid, pid, _ = topo.addr(c)
     return DstId(rid=rid, pnc=pid)
+
+
+def _common(topo, src, dsts):
+    allowed = topo.mask(src, dsts[0])
+    for d in dsts:
+        allowed &= topo.mask(src, d)
+    return _bits(allowed)
 
 
 def _plan(T, topo):
@@ -75,62 +83,73 @@ def _plan(T, topo):
     return ranks, classes, hubs
 
 
-def _hub(g, core, T, topo, ranks, cl, x, t):
-    allowed = topo.mask(core, ranks[0])
-    for d in ranks:
-        allowed &= topo.mask(core, d)
-    es = _spread(_bits(allowed))
-    g.wait_ge(T.sem.got, len(cl))
+def _hub_engines(topo, hub, ranks):
+    return len(_common(topo, hub, ranks)) // HUB_TRANSFERS
+
+
+def _hub(g, core, T, topo, ranks, classes, x, t):
+    es = _common(topo, core, ranks)
+    k = _hub_engines(topo, core, ranks)
+    nsrc = len(classes[x])
+    arrived = T.sem[("arra%d" if t < PA else "arrb%d") % x]
+    g.wait_ge(T.sem.got, nsrc)
     trs = []
     for i in range(HUB_TRANSFERS):
-        grp = ranks[i::HUB_TRANSFERS]
+        grp = []
+        for cl in classes:
+            grp += cl[i::HUB_TRANSFERS]
         m = 0
-        for e in es[i * HUB_ENGINES:(i + 1) * HUB_ENGINES]:
+        for e in es[i * k:(i + 1) * k]:
             m |= 1 << e
         trs.append(RemoteDMATransfer(
-            dst_ids=[_dst(topo, d) for d in grp], dma_engine_mask=m, remote_sem=T.sem["arr%d" % x],
-            srcs=[T.hin[i2] for i2 in range(len(cl))], dsts=[T.land[x * P + t] for _d in grp], alu_op=1))
+            dst_ids=[_dst(topo, d) for d in grp], dma_engine_mask=m, remote_sem=arrived,
+            srcs=[T.hin[j] for j in range(nsrc)], dsts=[T.land[x * P + t] for _d in grp], alu_op=1))
     g.remote_dma_fused(trs, local_sem=T.sem.sent)
-    g.wait_ge(T.sem.sent, HUB_TRANSFERS * HUB_ENGINES)
+    g.wait_ge(T.sem.sent, HUB_TRANSFERS * k)
 
 
-def _rank(g, core, T, topo, classes, hubs):
+def _rank(g, core, T, topo, ranks, classes, hubs):
     x = [i for i, cl in enumerate(classes) if core in cl][0]
     me = classes[x].index(core)
-    queues = [g.sync, g.scalar]
 
-    g.sync.dma_start(T.stage[0:PA], T.a[:, :]).then_inc(T.sem.ld, 16)
-    g.scalar.dma_start(T.stage[PA:P], T.b[:, :]).then_inc(T.sem.ld, 16)
+    g.scalar.dma_start(T.stage[PA:P], T.b[:, :]).then_inc(T.sem.ldb, 16)
+    g.sync.dma_start(T.stage[0:PA], T.a[:, :]).then_inc(T.sem.lda, 16)
 
-    g.wait_ge(T.sem.ld, 32)
-    allowed = topo.mask(core, hubs[x][0])
-    for h in hubs[x]:
-        allowed &= topo.mask(core, h)
-    es = _spread(_bits(allowed))
-    for t0 in range(0, P, RANK_TRANSFERS):
+    es = _spread(_common(topo, core, hubs[x]))
+
+    def send(ts):
         g.remote_dma_fused(
-            [RemoteDMATransfer(dst_ids=[_dst(topo, hubs[x][t])], dma_engine_mask=1 << es[t - t0],
+            [RemoteDMATransfer(dst_ids=[_dst(topo, hubs[x][t])], dma_engine_mask=1 << es[i],
                                remote_sem=T.sem.got, src=T.stage[t], dst=T.hin[me])
-             for t in range(t0, min(P, t0 + RANK_TRANSFERS))],
+             for i, t in enumerate(ts)],
             local_sem=T.sem.sent)
 
-    wa, wb = RPP * MDIM, RPP * FDIM
-    for c, q in enumerate(queues):
-        q.wait_ge(T.sem["arr%d" % c], P * HUB_ENGINES)
-        q.dma_start(T.sa[0:Q, c * wa:(c + 1) * wa], T.land[c * P:c * P + PA]).then_inc(T.sem["in%d" % c], 16)
-        q.dma_start(T.sb[0:Q, c * wb:(c + 1) * wb], T.land[c * P + PA:(c + 1) * P]).then_inc(T.sem["in%d" % c], 16)
+    g.wait_ge(T.sem.ldb, 16)
+    for t0 in range(PA, P, len(es)):
+        send(list(range(t0, min(P, t0 + len(es)))))
+    g.wait_ge(T.sem.lda, 16)
+    for t0 in range(0, PA, len(es)):
+        send(list(range(t0, min(PA, t0 + len(es)))))
 
-    terms = [(0, 0), (0, 1), (1, 0), (1, 1)]
-    g.tensor.wait_ge(T.sem.in0, 32)
-    n, last = 0, len(terms) * RPP
-    for (ca, cb) in terms:
-        if (ca, cb) == (0, 1):
-            g.tensor.wait_ge(T.sem.in1, 32)
+    wa, wb = RPP * MDIM, RPP * FDIM
+    for c, q in enumerate([g.sync, g.scalar]):
+        q.wait_ge(T.sem["arrb%d" % c], sum(_hub_engines(topo, h, ranks) for h in hubs[c][PA:P]))
+        q.dma_start(T.sb[0:Q, c * wb:(c + 1) * wb], T.land[c * P + PA:(c + 1) * P]).then_inc(T.sem["inb%d" % c], 16)
+        q.wait_ge(T.sem["arra%d" % c], sum(_hub_engines(topo, h, ranks) for h in hubs[c][0:PA]))
+        q.dma_start(T.sa[0:Q, c * wa:(c + 1) * wa], T.land[c * P:c * P + PA]).then_inc(T.sem["ina%d" % c], 16)
+
+    g.vector.wait_ge(T.sem.inb0, 16)
+    g.vector.wait_ge(T.sem.inb1, 16)
+    g.vector.tensor_tensor(T.sbs[0:Q, :], T.sb[0:Q, 0:wb], T.sb[0:Q, wb:2 * wb], AluOpType.add).then_inc(T.sem.bs, 1)
+    g.tensor.wait_ge(T.sem.bs, 1)
+    n, last = 0, 2 * RPP
+    for c in range(2):
+        g.tensor.wait_ge(T.sem["ina%d" % c], 16)
         for s in range(RPP):
             n += 1
             mm = g.tensor.matmul(T.ps[:, :],
-                                 T.sa[0:Q, ca * wa + s * MDIM:ca * wa + (s + 1) * MDIM],
-                                 T.sb[0:Q, cb * wb + s * FDIM:cb * wb + (s + 1) * FDIM],
+                                 T.sa[0:Q, c * wa + s * MDIM:c * wa + (s + 1) * MDIM],
+                                 T.sbs[0:Q, s * FDIM:(s + 1) * FDIM],
                                  n == 1, n == last)
     mm.then_inc(T.sem.mm, 1)
 
@@ -145,8 +164,8 @@ def _rank(g, core, T, topo, classes, hubs):
 def rank_program(g, core, T, topo):
     ranks, classes, hubs = _plan(T, topo)
     if T.rank_of(core) is not None:
-        _rank(g, core, T, topo, classes, hubs)
+        _rank(g, core, T, topo, ranks, classes, hubs)
         return
     for x, row in enumerate(hubs):
         if core in row:
-            _hub(g, core, T, topo, ranks, classes[x], x, row.index(core))
+            _hub(g, core, T, topo, ranks, classes, x, row.index(core))

from concourse.bass import DstId, RemoteDMATransfer
from concourse.mybir import AluOpType

KDIM, MDIM, FDIM = 128, 128, 32
W = 8
PA = KDIM * MDIM // (128 * W)
PB = KDIM * FDIM // (128 * W)
P = PA + PB
RPP = 2
Q = KDIM // RPP
HUB_TRANSFERS = 4
MAXSRC = 8

SCRATCH = {
    "stage": ("dram", [P, 128, W], "bfloat16"),
    "hin": ("dram", [MAXSRC, 128, W], "bfloat16"),
    "land": ("dram", [2 * P, 128, W], "bfloat16"),
    "sa": ("sbuf", [128, 2 * RPP * MDIM], "bfloat16"),
    "sb": ("sbuf", [128, 2 * RPP * FDIM], "bfloat16"),
    "sbs": ("sbuf", [128, RPP * FDIM], "bfloat16"),
    "ys": ("sbuf", [128, FDIM], "bfloat16"),
    "ps": ("psum", [128, FDIM], "float32"),
}
SEMAPHORES = ["lda", "ldb", "sent", "got", "arra0", "arra1", "arrb0", "arrb1",
              "ina0", "ina1", "inb0", "inb1", "bs", "mm", "cp", "st"]


def _bits(mask):
    return [e for e in range(mask.bit_length()) if (mask >> e) & 1]


def _spread(es):
    return es[0::2] + es[1::2]


def _dst(topo, c):
    rid, pid, _ = topo.addr(c)
    return DstId(rid=rid, pnc=pid)


def _common(topo, src, dsts):
    allowed = topo.mask(src, dsts[0])
    for d in dsts:
        allowed &= topo.mask(src, d)
    return _bits(allowed)


def _plan(T, topo):
    ranks = list(T.cores)
    classes = []
    for r in ranks:
        for cl in classes:
            if topo.may_write(cl[0], r) and topo.may_write(r, cl[0]):
                cl.append(r)
                break
        else:
            classes.append([r])

    def pair(ch):
        for o in range(topo.CHIPS):
            if topo.mates(ch, o):
                return min(ch, o)
        return ch

    slots, dies, hubs = [], {}, []
    for cl in classes:
        cand = [c for c in range(topo.CHIPS * topo.CORES_PER_CHIP)
                if c not in ranks
                and all(topo.may_write(s, c) for s in cl)
                and all(topo.may_write(c, d) for d in ranks)]
        row, chips = [], []
        for _t in range(P):
            best = min((c for c in cand if c not in row),
                       key=lambda c: (slots.count((pair(topo.chip(c)), topo.die(c))),
                                      chips.count(topo.chip(c)),
                                      sum(1 for u in slots if u[0] == pair(topo.chip(c))),
                                      dies.get(topo.die(c), 0), c))
            row.append(best)
            chips.append(topo.chip(best))
            slots.append((pair(topo.chip(best)), topo.die(best)))
            dies[topo.die(best)] = dies.get(topo.die(best), 0) + 1
        hubs.append(row)
    return ranks, classes, hubs


def _hub_engines(topo, hub, ranks):
    return len(_common(topo, hub, ranks)) // HUB_TRANSFERS


def _hub(g, core, T, topo, ranks, classes, x, t):
    es = _common(topo, core, ranks)
    k = _hub_engines(topo, core, ranks)
    nsrc = len(classes[x])
    arrived = T.sem[("arra%d" if t < PA else "arrb%d") % x]
    g.wait_ge(T.sem.got, nsrc)
    trs = []
    for i in range(HUB_TRANSFERS):
        grp = []
        for cl in classes:
            grp += cl[i::HUB_TRANSFERS]
        m = 0
        for e in es[i * k:(i + 1) * k]:
            m |= 1 << e
        trs.append(RemoteDMATransfer(
            dst_ids=[_dst(topo, d) for d in grp], dma_engine_mask=m, remote_sem=arrived,
            srcs=[T.hin[j] for j in range(nsrc)], dsts=[T.land[x * P + t] for _d in grp], alu_op=1))
    g.remote_dma_fused(trs, local_sem=T.sem.sent)
    g.wait_ge(T.sem.sent, HUB_TRANSFERS * k)


def _rank(g, core, T, topo, ranks, classes, hubs):
    x = [i for i, cl in enumerate(classes) if core in cl][0]
    me = classes[x].index(core)

    g.scalar.dma_start(T.stage[PA:P], T.b[:, :]).then_inc(T.sem.ldb, 16)
    g.sync.dma_start(T.stage[0:PA], T.a[:, :]).then_inc(T.sem.lda, 16)

    es = _spread(_common(topo, core, hubs[x]))

    def send(ts):
        g.remote_dma_fused(
            [RemoteDMATransfer(dst_ids=[_dst(topo, hubs[x][t])], dma_engine_mask=1 << es[i],
                               remote_sem=T.sem.got, src=T.stage[t], dst=T.hin[me])
             for i, t in enumerate(ts)],
            local_sem=T.sem.sent)

    g.wait_ge(T.sem.ldb, 16)
    for t0 in range(PA, P, len(es)):
        send(list(range(t0, min(P, t0 + len(es)))))
    g.wait_ge(T.sem.lda, 16)
    for t0 in range(0, PA, len(es)):
        send(list(range(t0, min(PA, t0 + len(es)))))

    wa, wb = RPP * MDIM, RPP * FDIM
    for c, q in enumerate([g.sync, g.scalar]):
        q.wait_ge(T.sem["arrb%d" % c], sum(_hub_engines(topo, h, ranks) for h in hubs[c][PA:P]))
        q.dma_start(T.sb[0:Q, c * wb:(c + 1) * wb], T.land[c * P + PA:(c + 1) * P]).then_inc(T.sem["inb%d" % c], 16)
        q.wait_ge(T.sem["arra%d" % c], sum(_hub_engines(topo, h, ranks) for h in hubs[c][0:PA]))
        q.dma_start(T.sa[0:Q, c * wa:(c + 1) * wa], T.land[c * P:c * P + PA]).then_inc(T.sem["ina%d" % c], 16)

    g.vector.wait_ge(T.sem.inb0, 16)
    g.vector.wait_ge(T.sem.inb1, 16)
    g.vector.tensor_tensor(T.sbs[0:Q, :], T.sb[0:Q, 0:wb], T.sb[0:Q, wb:2 * wb], AluOpType.add).then_inc(T.sem.bs, 1)
    g.tensor.wait_ge(T.sem.bs, 1)
    n, last = 0, 2 * RPP
    for c in range(2):
        g.tensor.wait_ge(T.sem["ina%d" % c], 16)
        for s in range(RPP):
            n += 1
            mm = g.tensor.matmul(T.ps[:, :],
                                 T.sa[0:Q, c * wa + s * MDIM:c * wa + (s + 1) * MDIM],
                                 T.sbs[0:Q, s * FDIM:(s + 1) * FDIM],
                                 n == 1, n == last)
    mm.then_inc(T.sem.mm, 1)

    g.vector.wait_ge(T.sem.mm, 1)
    g.vector.tensor_copy(T.ys[:, :], T.ps[:, :]).then_inc(T.sem.cp, 1)
    g.sync.wait_ge(T.sem.cp, 1)
    g.sync.dma_start(T.y[:, :], T.ys[:, :]).then_inc(T.sem.st, 16)
    g.sync.wait_ge(T.sem.st, 16)
    g.wait_ge(T.sem.sent, P)


def rank_program(g, core, T, topo):
    ranks, classes, hubs = _plan(T, topo)
    if T.rank_of(core) is not None:
        _rank(g, core, T, topo, ranks, classes, hubs)
        return
    for x, row in enumerate(hubs):
        if core in row:
            _hub(g, core, T, topo, ranks, classes, x, row.index(core))
